import numpy as np
import ml_dtypes


def mxq(x, axis, fmt="e4m3"):
    dtype, down = {"e4m3": (ml_dtypes.float8_e4m3fn, 7), "e5m2": (ml_dtypes.float8_e5m2, 14)}[fmt]
    v = np.moveaxis(np.asarray(x, np.float32).astype(ml_dtypes.bfloat16).astype(np.float64), axis, -1)
    blocks = v.reshape(v.shape[:-1] + (-1, 32))
    amax = np.abs(blocks).max(-1, keepdims=True)
    byte = np.maximum(np.where(amax > 0, np.frexp(amax)[1] - 1 + 127, 0) - down, 1)
    scale = np.exp2(byte - 127.0)
    codes = (blocks / scale).astype(np.float32).astype(dtype).astype(np.float64)
    return np.moveaxis((codes * scale).reshape(v.shape), -1, axis)


WIDE = False


def mx_kscale(k):
    if not WIDE:
        return np.ones(k)
    levels = np.array([10, -10, 5, -5, 0])
    if k % 512:
        return np.exp2(np.random.permutation(np.resize(levels, k // 32))).repeat(32)
    a = np.empty((k // 512, 16))
    for p in range(k // 512):
        a[p, :8] = np.random.permutation(np.resize(levels, 8))
        for g in range(8):
            far = levels[np.abs(levels - a[p, g]) >= 10]
            a[p, g + 8] = far[np.random.randint(len(far))]
    return np.exp2(a.ravel()).repeat(32)


def f64(x):
    return np.asarray(x).astype(np.float64)


def striped(idx):
    return np.tile(idx.reshape(-1, 16).T, (8, 1)).astype(np.uint16)


def unstriped(offs):
    return offs[:16].T.reshape(-1).astype(np.int64)


def pack_weight(w):
    k, n = w.shape
    w = f64(np.asarray(w, np.float32).astype(ml_dtypes.bfloat16)).reshape(k // 32, 32, n)
    amax = np.abs(w).max(1)
    byte = np.clip(np.where(amax > 0, np.frexp(amax)[1] - 1 + 127 - 7, 1), 1, 254)
    scaled = (w * np.exp2(127.0 - byte)[:, None, :]).reshape(k, n).astype(np.float32)
    words = np.ascontiguousarray(scaled.reshape(k // 512, 128, 4, n).transpose(0, 1, 3, 2)).astype(ml_dtypes.float8_e4m3fn).view(np.uint8)
    return words, np.ascontiguousarray(byte.astype(np.uint8).reshape(k // 512, 16, n))


def unpack_weight(words, scales):
    g, p, n, _ = words.shape
    vals = np.ascontiguousarray(words).view(ml_dtypes.float8_e4m3fn).astype(np.float64) * np.repeat(np.exp2(scales.astype(np.float64) - 127.0), 8, axis=1)[..., None]
    return vals.transpose(0, 1, 3, 2).reshape(g * 512, n)


def relu(v):
    return np.maximum(v, 0.0)


def sigmoid(v):
    return 1.0 / (1.0 + np.exp(-np.maximum(v, -700.0)))


K, T, S, D, N = 512, 2048, 512, 4, 256


def setup_inputs():
    n = np.random.standard_normal
    s = mx_kscale(K)[:, None]
    packed_xT = pack_weight(n((K, T)) * s)
    return {
        "x_words": packed_xT[0],
        "x_scales": packed_xT[1],
        "w1": (n((K, N)) / np.sqrt(K) / s).astype(np.float32),
        "lm": (np.random.uniform(0.3, 1.0, (N, 1))).astype(np.float32),
        "sc": (np.random.uniform(0.4, 0.8, (N, 1))).astype(np.float32),
        "offs": striped(np.random.permutation(T)[:S]),
    }


def reference(x_words, x_scales, w1, lm, sc, offs):
    xq = unpack_weight(x_words, x_scales)[:, unstriped(offs)]
    y = mxq(f64(w1), 0, "e4m3").T @ xq
    bl = y + f64(lm)
    gg = f64(sc) * ((relu(bl)) ** 2)
    mg = gg.reshape(len(gg), -1, D).max(axis=2)
    pk = np.repeat(mg, D, axis=1)
    on = (sigmoid(8.0 * (gg - pk + 0.1))) * (sigmoid(4.0 * (gg - 0.5)))
    return y - (on * (f64(sc) * bl))

@@ -1,0 +1,136 @@
+from contextlib import ExitStack
+
+import concourse.mybir as mybir
+
+K, T, S, D, N = 512, 2048, 512, 4, 256
+FLOPS = 2 * K * N * S
+
+F32 = mybir.dt.float32
+BF16 = mybir.dt.bfloat16
+I32 = mybir.dt.int32
+U32 = mybir.dt.uint32
+U16 = mybir.dt.uint16
+U8 = mybir.dt.uint8
+FP8X4 = mybir.dt.float8_e4m3fn_x4
+ALU = mybir.AluOpType
+ACT = mybir.ActivationFunctionType
+AX = mybir.AxisListType
+
+P = 128
+HALF = 256
+GG_ON_SCALAR = (1, 2, 3)
+
+
+def tile_picked_yspike_rest_p_kernel(tc, x_words, x_scales, w1, lm, sc, offs, out):
+    nc = tc.nc
+    with ExitStack() as ctx:
+        keep = ctx.enter_context(tc.tile_pool(name="keep", bufs=1))
+        psum = ctx.enter_context(tc.psum_pool(name="psum", bufs=1))
+
+        offsets = keep.tile([P, S // 16], U16, name="offsets")
+        w_raw = keep.tile([P, 4, N], F32, name="w_raw")
+        x_tab = keep.tile([P, T], I32, name="x_tab", align_bytes=64)
+        s_tab = keep.tile([P, T], U8, name="s_tab", align_bytes=64)
+        lm_col = keep.tile([P, 2], F32, name="lm_col")
+        sc_col = keep.tile([P, 2], F32, name="sc_col")
+
+        nc.vector.memset(s_tab[:].bitcast(I32), 0)
+        with nc.allow_non_contiguous_dma(reason="one value a partition"):
+            nc.scalar.dma_start(lm_col[:], lm.rearrange("(t p) o -> p (t o)", p=P))
+        nc.sync.dma_start(w_raw[:], w1.rearrange("(p j) m -> p j m", j=4))
+        nc.sync.dma_start(offsets[:], offs)
+        s_rows = x_scales[0].rearrange("(q r) c -> r q c", r=4)
+        for r in range(4):
+            nc.sync.dma_start(s_tab[r:P:32, :].bitcast(I32), s_rows[r].bitcast(I32))
+        nc.sync.dma_start(x_tab[:], x_words[0].rearrange("p c t -> p (c t)").bitcast(I32))
+        with nc.allow_non_contiguous_dma(reason="one value a partition"):
+            nc.sync.dma_start(sc_col[:], sc.rearrange("(t p) o -> p (t o)", p=P))
+
+        w_bf = keep.tile([P, N, 4], BF16, name="w_bf", align_bytes=64)
+        w_codes = keep.tile([P, N], U32, name="w_codes", align_bytes=64)
+        w_scales = keep.tile([P, N], U8, name="w_scales", align_bytes=64)
+        nc.scalar.copy(w_bf[:].rearrange("p (c i) j -> p c j i", i=4), w_raw[:].rearrange("p j (c i) -> p c j i", i=4))
+        s_pick = keep.tile([P, S], U8, name="s_pick", align_bytes=64)
+        nc.vector.tensor_copy(s_pick[:], s_tab[:].indirect(offsets[:]))
+        nc.vector.quantize_mx(out=w_codes[:].bitcast(FP8X4), scales=w_scales[:], in_=w_bf[:].rearrange("p m j -> p (m j)"))
+
+        x_pick = [keep.tile([P, HALF], U32, name="x_pick%d" % h, align_bytes=64) for h in range(2)]
+        chunks = [(h, t) for h in range(2) for t in range(2)]
+        y = {}
+        for h in range(2):
+            nc.vector.tensor_copy(x_pick[h][:], x_tab[:].bitcast(U32).indirect(offsets[:, 16 * h : 16 * (h + 1)]))
+            for t in range(2):
+                y[h, t] = psum.tile([P, HALF], F32, name="y%d%d" % (h, t))
+                nc.tensor.matmul_mx(
+                    out=y[h, t][:],
+                    lhsT=w_codes[:, P * t : P * (t + 1)].bitcast(FP8X4),
+                    lhsT_scale=w_scales[:, P * t : P * (t + 1)],
+                    rhs=x_pick[h][:].bitcast(FP8X4),
+                    rhs_scale=s_pick[:, HALF * h : HALF * (h + 1)],
+                    start=True,
+                    stop=True,
+                )
+
+        def buf(name, c, width=HALF):
+            return keep.tile([P, width], F32, name="%s%d" % (name, c))
+
+        st = [dict() for c in chunks]
+
+        def gain(c):
+            h, t = chunks[c]
+            r = buf("r", c)
+            gg = buf("gg", c)
+            nc.scalar.activation(r[:], y[h, t][:], ACT.Relu, bias=lm_col[:, t : t + 1])
+            if c in GG_ON_SCALAR:
+                q = buf("q", c)
+                nc.scalar.activation(q[:], r[:], ACT.Square)
+                nc.scalar.activation(gg[:], q[:], ACT.Copy, scale=sc_col[:, t : t + 1])
+            else:
+                nc.vector.scalar_tensor_tensor(gg[:], r[:], sc_col[:, t : t + 1], r[:], ALU.mult, ALU.mult)
+            st[c].update(gg=gg)
+
+        def peak(c):
+            gg = st[c]["gg"]
+            mg = buf("mg", c, HALF // D)
+            s2 = buf("s2", c)
+            nc.vector.tensor_reduce(mg[:], gg[:].rearrange("p (v d) -> p v d", d=D), AX.X, ALU.max)
+            nc.scalar.activation(s2[:], gg[:], ACT.Sigmoid, bias=-2.0, scale=4.0)
+            st[c].update(mg=mg, s2=s2)
+
+        def gap(c):
+            gg, mg = st[c]["gg"], st[c]["mg"]
+            d = buf("d", c)
+            s1 = buf("s1", c)
+            nc.vector.tensor_tensor(
+                d[:].rearrange("p (v d) -> p v d", d=D),
+                gg[:].rearrange("p (v d) -> p v d", d=D),
+                mg[:].unsqueeze(2).to_broadcast([P, HALF // D, D]),
+                ALU.subtract,
+            )
+            nc.scalar.activation(s1[:], d[:], ACT.Sigmoid, bias=0.8, scale=8.0)
+            st[c].update(s1=s1)
+
+        def gate2(c):
+            h, t = chunks[c]
+            u = buf("u", c)
+            nc.vector.scalar_tensor_tensor(u[:], y[h, t][:], lm_col[:, t : t + 1], st[c]["s2"][:], ALU.add, ALU.mult)
+            st[c].update(u=u)
+
+        def gate1(c):
+            h, t = chunks[c]
+            z = buf("z", c)
+            nc.vector.scalar_tensor_tensor(z[:], st[c]["u"][:], sc_col[:, t : t + 1], st[c]["s1"][:], ALU.mult, ALU.mult)
+            st[c].update(z=z)
+
+        def rest(c):
+            h, t = chunks[c]
+            o = buf("o", c)
+            nc.vector.tensor_tensor(o[:], y[h, t][:], st[c]["z"][:], ALU.subtract)
+            nc.sync.dma_start(out[P * t : P * (t + 1), HALF * h : HALF * (h + 1)], o[:])
+
+        stages = [gain, peak, gap, gate2, gate1, rest]
+        for step in range(len(chunks) + len(stages) - 1):
+            for s in reversed(range(len(stages))):
+                c = step - s
+                if 0 <= c < len(chunks):
+                    stages[s](c)

@@ -18,7 +18,7 @@ AX = mybir.AxisListType
 
 P = 128
 HALF = 256
-GG_ON_SCALAR = (1, 2, 3)
+GG_ON_SCALAR = ()
 
 
 def tile_picked_yspike_rest_p_kernel(tc, x_words, x_scales, w1, lm, sc, offs, out):
@@ -30,11 +30,16 @@ def tile_picked_yspike_rest_p_kernel(tc, x_words, x_scales, w1, lm, sc, offs, ou
         offsets = keep.tile([P, S // 16], U16, name="offsets")
         w_raw = keep.tile([P, 4, N], F32, name="w_raw")
         x_tab = keep.tile([P, T], I32, name="x_tab", align_bytes=64)
-        s_tab = keep.tile([P, T], U8, name="s_tab", align_bytes=64)
+        s_tab = keep.tile([P, T], U8, name="s_tab", tag="scale_slot", align_bytes=64)
         lm_col = keep.tile([P, 2], F32, name="lm_col")
         sc_col = keep.tile([P, 2], F32, name="sc_col")
 
+        warm_in = keep.tile([P, 1], F32, name="warm_in")
+        warm_out = keep.tile([P, 1], F32, name="warm_out")
         nc.vector.memset(s_tab[:].bitcast(I32), 0)
+        nc.vector.memset(warm_in[:], 0.0)
+        nc.scalar.activation(warm_out[:], warm_in[:], ACT.Sigmoid)
+
         with nc.allow_non_contiguous_dma(reason="one value a partition"):
             nc.scalar.dma_start(lm_col[:], lm.rearrange("(t p) o -> p (t o)", p=P))
         nc.sync.dma_start(w_raw[:], w1.rearrange("(p j) m -> p j m", j=4))
@@ -48,12 +53,14 @@ def tile_picked_yspike_rest_p_kernel(tc, x_words, x_scales, w1, lm, sc, offs, ou
 
         w_bf = keep.tile([P, N, 4], BF16, name="w_bf", align_bytes=64)
         w_codes = keep.tile([P, N], U32, name="w_codes", align_bytes=64)
-        w_scales = keep.tile([P, N], U8, name="w_scales", align_bytes=64)
         nc.scalar.copy(w_bf[:].rearrange("p (c i) j -> p c j i", i=4), w_raw[:].rearrange("p j (c i) -> p c j i", i=4))
         s_pick = keep.tile([P, S], U8, name="s_pick", align_bytes=64)
         nc.vector.tensor_copy(s_pick[:], s_tab[:].indirect(offsets[:]))
+        w_scales = keep.tile([P, N], U8, name="w_scales", tag="scale_slot", align_bytes=64)
         nc.vector.quantize_mx(out=w_codes[:].bitcast(FP8X4), scales=w_scales[:], in_=w_bf[:].rearrange("p m j -> p (m j)"))
 
+        neg_lm = keep.tile([P, 2], F32, name="neg_lm")
+        nc.vector.tensor_scalar(neg_lm[:], lm_col[:], -1.0, None, ALU.mult)
         x_pick = [keep.tile([P, HALF], U32, name="x_pick%d" % h, align_bytes=64) for h in range(2)]
         chunks = [(h, t) for h in range(2) for t in range(2)]
         y = {}
@@ -76,38 +83,54 @@ def tile_picked_yspike_rest_p_kernel(tc, x_words, x_scales, w1, lm, sc, offs, ou
 
         st = [dict() for c in chunks]
 
-        def gain(c):
+        def relu(c):
             h, t = chunks[c]
             r = buf("r", c)
-            gg = buf("gg", c)
             nc.scalar.activation(r[:], y[h, t][:], ACT.Relu, bias=lm_col[:, t : t + 1])
-            if c in GG_ON_SCALAR:
-                q = buf("q", c)
-                nc.scalar.activation(q[:], r[:], ACT.Square)
-                nc.scalar.activation(gg[:], q[:], ACT.Copy, scale=sc_col[:, t : t + 1])
-            else:
-                nc.vector.scalar_tensor_tensor(gg[:], r[:], sc_col[:, t : t + 1], r[:], ALU.mult, ALU.mult)
+            st[c].update(r=r)
+
+        def square(c):
+            q = buf("q", c)
+            nc.scalar.activation(q[:], st[c]["r"][:], ACT.Square)
+            st[c].update(q=q)
+
+        def gain_s(c):
+            h, t = chunks[c]
+            gg = buf("gg", c)
+            nc.scalar.activation(gg[:], st[c]["q"][:], ACT.Copy, scale=sc_col[:, t : t + 1])
+            st[c].update(gg=gg)
+
+        def gain_v(c):
+            h, t = chunks[c]
+            gg = buf("gg", c)
+            r = st[c]["r"]
+            nc.vector.scalar_tensor_tensor(gg[:], r[:], sc_col[:, t : t + 1], r[:], ALU.mult, ALU.mult)
             st[c].update(gg=gg)
 
         def peak(c):
-            gg = st[c]["gg"]
             mg = buf("mg", c, HALF // D)
+            nc.vector.tensor_reduce(mg[:], st[c]["gg"][:].rearrange("p (v d) -> p v d", d=D), AX.X, ALU.max)
+            st[c].update(mg=mg)
+
+        def sig2(c):
             s2 = buf("s2", c)
-            nc.vector.tensor_reduce(mg[:], gg[:].rearrange("p (v d) -> p v d", d=D), AX.X, ALU.max)
-            nc.scalar.activation(s2[:], gg[:], ACT.Sigmoid, bias=-2.0, scale=4.0)
-            st[c].update(mg=mg, s2=s2)
+            nc.scalar.activation(s2[:], st[c]["gg"][:], ACT.Sigmoid, bias=-2.0, scale=4.0)
+            st[c].update(s2=s2)
 
         def gap(c):
             gg, mg = st[c]["gg"], st[c]["mg"]
             d = buf("d", c)
-            s1 = buf("s1", c)
             nc.vector.tensor_tensor(
                 d[:].rearrange("p (v d) -> p v d", d=D),
                 gg[:].rearrange("p (v d) -> p v d", d=D),
                 mg[:].unsqueeze(2).to_broadcast([P, HALF // D, D]),
                 ALU.subtract,
             )
-            nc.scalar.activation(s1[:], d[:], ACT.Sigmoid, bias=0.8, scale=8.0)
+            st[c].update(d=d)
+
+        def sig1(c):
+            s1 = buf("s1", c)
+            nc.scalar.activation(s1[:], st[c]["d"][:], ACT.Sigmoid, bias=0.8, scale=8.0)
             st[c].update(s1=s1)
 
         def gate2(c):
@@ -122,15 +145,41 @@ def tile_picked_yspike_rest_p_kernel(tc, x_words, x_scales, w1, lm, sc, offs, ou
             nc.vector.scalar_tensor_tensor(z[:], st[c]["u"][:], sc_col[:, t : t + 1], st[c]["s1"][:], ALU.mult, ALU.mult)
             st[c].update(z=z)
 
+        def gate1g(c):
+            z = buf("z", c)
+            nc.gpsimd.tensor_tensor(z[:], st[c]["u"][:], st[c]["s1"][:], ALU.mult)
+            st[c].update(z=z)
+
         def rest(c):
             h, t = chunks[c]
             o = buf("o", c)
             nc.vector.tensor_tensor(o[:], y[h, t][:], st[c]["z"][:], ALU.subtract)
             nc.sync.dma_start(out[P * t : P * (t + 1), HALF * h : HALF * (h + 1)], o[:])
 
-        stages = [gain, peak, gap, gate2, gate1, rest]
-        for step in range(len(chunks) + len(stages) - 1):
-            for s in reversed(range(len(stages))):
-                c = step - s
-                if 0 <= c < len(chunks):
-                    stages[s](c)
+        def shift(c):
+            h, t = chunks[c]
+            bl = buf("bl", c)
+            nc.scalar.activation(bl[:], y[h, t][:], ACT.Identity, bias=lm_col[:, t : t + 1])
+            st[c].update(bl=bl)
+
+        def fire(c):
+            h, t = chunks[c]
+            on = buf("on", c)
+            nc.vector.scalar_tensor_tensor(on[:], st[c]["s1"][:], sc_col[:, t : t + 1], st[c]["s2"][:], ALU.mult, ALU.mult)
+            st[c].update(on=on)
+
+        def keepbl(c):
+            p = buf("p", c)
+            nc.vector.scalar_tensor_tensor(p[:], st[c]["on"][:], 1.0, st[c]["bl"][:], ALU.subtract, ALU.mult)
+            st[c].update(p=p)
+
+        def unshift(c):
+            h, t = chunks[c]
+            o = buf("o", c)
+            nc.scalar.activation(o[:], st[c]["p"][:], ACT.Identity, bias=neg_lm[:, t : t + 1], scale=-1.0)
+            nc.sync.dma_start(out[P * t : P * (t + 1), HALF * h : HALF * (h + 1)], o[:])
+
+        A, B = (0, 1), (2, 3)
+        for stage, group in [(relu, A), (gain_v, A), (relu, B), (peak, A), (square, B), (gap, A), (gain_s, B), (peak, B), (sig2, A), (gap, B), (sig1, A), (fire, A), (shift, A), (keepbl, A), (sig2, B), (gate2, B), (sig1, B), (gate1, B), (unshift, A), (rest, B)]:
+            for c in group:
+                stage(c)

@@ -40,27 +40,26 @@ def tile_picked_yspike_rest_p_kernel(tc, x_words, x_scales, w1, lm, sc, offs, ou
         nc.vector.memset(warm_in[:], 0.0)
         nc.scalar.activation(warm_out[:], warm_in[:], ACT.Sigmoid)
 
-        with nc.allow_non_contiguous_dma(reason="one value a partition"):
-            nc.scalar.dma_start(lm_col[:], lm.rearrange("(t p) o -> p (t o)", p=P))
         nc.sync.dma_start(w_raw[:], w1.rearrange("(p j) m -> p j m", j=4))
         nc.sync.dma_start(offsets[:], offs)
         s_rows = x_scales[0].rearrange("(q r) c -> r q c", r=4)
         for r in range(4):
             nc.sync.dma_start(s_tab[r:P:32, :].bitcast(I32), s_rows[r].bitcast(I32))
         nc.sync.dma_start(x_tab[:], x_words[0].rearrange("p c t -> p (c t)").bitcast(I32))
-        with nc.allow_non_contiguous_dma(reason="one value a partition"):
-            nc.sync.dma_start(sc_col[:], sc.rearrange("(t p) o -> p (t o)", p=P))
+        nc.sync.dma_start(lm_col[:], lm.rearrange("(p t) o -> p (t o)", t=2))
+        nc.sync.dma_start(sc_col[:], sc.rearrange("(p t) o -> p (t o)", t=2))
 
         w_bf = keep.tile([P, N, 4], BF16, name="w_bf", align_bytes=64)
         w_codes = keep.tile([P, N], U32, name="w_codes", align_bytes=64)
-        nc.scalar.copy(w_bf[:].rearrange("p (c i) j -> p c j i", i=4), w_raw[:].rearrange("p j (c i) -> p c j i", i=4))
+        nc.scalar.copy(w_bf[:].rearrange("p (t c i) j -> p c j i t", t=2, i=2), w_raw[:].rearrange("p j (c i t) -> p c j i t", i=2, t=2))
         s_pick = keep.tile([P, S], U8, name="s_pick", align_bytes=64)
         nc.vector.tensor_copy(s_pick[:], s_tab[:].indirect(offsets[:]))
         w_scales = keep.tile([P, N], U8, name="w_scales", tag="scale_slot", align_bytes=64)
         nc.vector.quantize_mx(out=w_codes[:].bitcast(FP8X4), scales=w_scales[:], in_=w_bf[:].rearrange("p m j -> p (m j)"))
 
         neg_lm = keep.tile([P, 2], F32, name="neg_lm")
-        nc.vector.tensor_scalar(neg_lm[:], lm_col[:], -1.0, None, ALU.mult)
+        nc.scalar.activation(neg_lm[:], lm_col[:], ACT.Copy, scale=-1.0)
+        out_rows = out.rearrange("(p t) j -> t p j", t=2)
         x_pick = [keep.tile([P, HALF], U32, name="x_pick%d" % h, align_bytes=64) for h in range(2)]
         chunks = [(h, t) for h in range(2) for t in range(2)]
         y = {}
@@ -154,7 +153,7 @@ def tile_picked_yspike_rest_p_kernel(tc, x_words, x_scales, w1, lm, sc, offs, ou
             h, t = chunks[c]
             o = buf("o", c)
             nc.vector.tensor_tensor(o[:], y[h, t][:], st[c]["z"][:], ALU.subtract)
-            nc.sync.dma_start(out[P * t : P * (t + 1), HALF * h : HALF * (h + 1)], o[:])
+            nc.sync.dma_start(out_rows[t][:, HALF * h : HALF * (h + 1)], o[:])
 
         def shift(c):
             h, t = chunks[c]
@@ -177,7 +176,7 @@ def tile_picked_yspike_rest_p_kernel(tc, x_words, x_scales, w1, lm, sc, offs, ou
             h, t = chunks[c]
             o = buf("o", c)
             nc.scalar.activation(o[:], st[c]["p"][:], ACT.Identity, bias=neg_lm[:, t : t + 1], scale=-1.0)
-            nc.sync.dma_start(out[P * t : P * (t + 1), HALF * h : HALF * (h + 1)], o[:])
+            nc.sync.dma_start(out_rows[t][:, HALF * h : HALF * (h + 1)], o[:])
 
         A, B = (0, 1), (2, 3)
         for stage, group in [(relu, A), (gain_v, A), (relu, B), (peak, A), (square, B), (gap, A), (gain_s, B), (peak, B), (sig2, A), (gap, B), (sig1, A), (fire, A), (shift, A), (keepbl, A), (sig2, B), (gate2, B), (sig1, B), (gate1, B), (unshift, A), (rest, B)]:

@@ -17,8 +17,17 @@ ACT = mybir.ActivationFunctionType
 AX = mybir.AxisListType
 
 P = 128
-HALF = 256
-GG_ON_SCALAR = ()
+PACK = 4
+QUADRANT = 32
+SCALE_ROWS = 4
+TILES = N // P
+HALVES = 2
+WIDTH = S // HALVES
+GROUPS = WIDTH // D
+LIST_ROWS = 16
+LIST_COLUMNS = WIDTH // LIST_ROWS
+NEIGHBOURS = 2
+MX_ALIGN = 64
 
 
 def tile_picked_yspike_rest_p_kernel(tc, x_words, x_scales, w1, lm, sc, offs, out):
@@ -27,158 +36,161 @@ def tile_picked_yspike_rest_p_kernel(tc, x_words, x_scales, w1, lm, sc, offs, ou
         keep = ctx.enter_context(tc.tile_pool(name="keep", bufs=1))
         psum = ctx.enter_context(tc.psum_pool(name="psum", bufs=1))
 
-        offsets = keep.tile([P, S // 16], U16, name="offsets")
-        w_raw = keep.tile([P, 4, N], F32, name="w_raw")
-        x_tab = keep.tile([P, T], I32, name="x_tab", align_bytes=64)
-        s_tab = keep.tile([P, T], U8, name="s_tab", tag="scale_slot", align_bytes=64)
-        lm_col = keep.tile([P, 2], F32, name="lm_col")
-        sc_col = keep.tile([P, 2], F32, name="sc_col")
-
+        offsets = keep.tile([P, S // LIST_ROWS], U16, name="offsets")
+        w_raw = keep.tile([P, PACK, N], F32, name="w_raw")
+        x_table = keep.tile([P, T], I32, name="x_table", align_bytes=MX_ALIGN)
+        scale_table = keep.tile([P, T], U8, name="scale_table", tag="scale_slot", align_bytes=MX_ALIGN)
+        lm_col = keep.tile([P, TILES], F32, name="lm_col")
+        sc_col = keep.tile([P, TILES], F32, name="sc_col")
         warm_in = keep.tile([P, 1], F32, name="warm_in")
         warm_out = keep.tile([P, 1], F32, name="warm_out")
-        nc.vector.memset(s_tab[:].bitcast(I32), 0)
+
+        nc.vector.memset(scale_table[:].bitcast(I32), 0)
+
         nc.vector.memset(warm_in[:], 0.0)
         nc.scalar.activation(warm_out[:], warm_in[:], ACT.Sigmoid)
 
-        nc.sync.dma_start(w_raw[:], w1.rearrange("(p j) m -> p j m", j=4))
+        nc.sync.dma_start(w_raw[:], w1.rearrange("(p j) m -> p j m", j=PACK))
         nc.sync.dma_start(offsets[:], offs)
-        s_rows = x_scales[0].rearrange("(q r) c -> r q c", r=4)
-        for r in range(4):
-            nc.sync.dma_start(s_tab[r:P:32, :].bitcast(I32), s_rows[r].bitcast(I32))
-        nc.sync.dma_start(x_tab[:], x_words[0].rearrange("p c t -> p (c t)").bitcast(I32))
-        nc.sync.dma_start(lm_col[:], lm.rearrange("(p t) o -> p (t o)", t=2))
-        nc.sync.dma_start(sc_col[:], sc.rearrange("(p t) o -> p (t o)", t=2))
+        scale_rows = x_scales[0].rearrange("(q r) c -> r q c", r=SCALE_ROWS)
+        for r in range(SCALE_ROWS):
+            nc.sync.dma_start(scale_table[r:P:QUADRANT, :].bitcast(I32), scale_rows[r].bitcast(I32))
+        nc.sync.dma_start(x_table[:], x_words[0].rearrange("p c j -> p (c j)").bitcast(I32))
+        nc.sync.dma_start(lm_col[:], lm.rearrange("(p t) o -> p (t o)", t=TILES))
+        nc.sync.dma_start(sc_col[:], sc.rearrange("(p t) o -> p (t o)", t=TILES))
 
-        w_bf = keep.tile([P, N, 4], BF16, name="w_bf", align_bytes=64)
-        w_codes = keep.tile([P, N], U32, name="w_codes", align_bytes=64)
-        nc.scalar.copy(w_bf[:].rearrange("p (t c i) j -> p c j i t", t=2, i=2), w_raw[:].rearrange("p j (c i t) -> p c j i t", i=2, t=2))
-        s_pick = keep.tile([P, S], U8, name="s_pick", align_bytes=64)
-        nc.vector.tensor_copy(s_pick[:], s_tab[:].indirect(offsets[:]))
-        w_scales = keep.tile([P, N], U8, name="w_scales", tag="scale_slot", align_bytes=64)
-        nc.vector.quantize_mx(out=w_codes[:].bitcast(FP8X4), scales=w_scales[:], in_=w_bf[:].rearrange("p m j -> p (m j)"))
+        w_bf = keep.tile([P, N, PACK], BF16, name="w_bf", align_bytes=MX_ALIGN)
+        w_codes = keep.tile([P, N], U32, name="w_codes", align_bytes=MX_ALIGN)
+        nc.scalar.copy(
+            w_bf[:].rearrange("p (t g i) j -> p g j i t", t=TILES, i=NEIGHBOURS),
+            w_raw[:].rearrange("p j (g i t) -> p g j i t", t=TILES, i=NEIGHBOURS),
+        )
+        scale_pick = keep.tile([P, S], U8, name="scale_pick", align_bytes=MX_ALIGN)
+        nc.vector.tensor_copy(scale_pick[:], scale_table[:].indirect(offsets[:]))
 
-        neg_lm = keep.tile([P, 2], F32, name="neg_lm")
+        w_scales = keep.tile([P, N], U8, name="w_scales", tag="scale_slot", align_bytes=MX_ALIGN)
+        nc.vector.quantize_mx(
+            out=w_codes[:].bitcast(FP8X4), scales=w_scales[:], in_=w_bf[:].rearrange("p m j -> p (m j)")
+        )
+
+        neg_lm = keep.tile([P, TILES], F32, name="neg_lm")
         nc.scalar.activation(neg_lm[:], lm_col[:], ACT.Copy, scale=-1.0)
-        out_rows = out.rearrange("(p t) j -> t p j", t=2)
-        x_pick = [keep.tile([P, HALF], U32, name="x_pick%d" % h, align_bytes=64) for h in range(2)]
-        chunks = [(h, t) for h in range(2) for t in range(2)]
+
+        x_pick = [keep.tile([P, WIDTH], U32, name="x_pick%d" % h, align_bytes=MX_ALIGN) for h in range(HALVES)]
         y = {}
-        for h in range(2):
-            nc.vector.tensor_copy(x_pick[h][:], x_tab[:].bitcast(U32).indirect(offsets[:, 16 * h : 16 * (h + 1)]))
-            for t in range(2):
-                y[h, t] = psum.tile([P, HALF], F32, name="y%d%d" % (h, t))
+        for h in range(HALVES):
+            half_list = offsets[:, LIST_COLUMNS * h : LIST_COLUMNS * (h + 1)]
+            nc.vector.tensor_copy(x_pick[h][:], x_table[:].bitcast(U32).indirect(half_list))
+            for t in range(TILES):
+                y[h, t] = psum.tile([P, WIDTH], F32, name="y%d%d" % (h, t))
                 nc.tensor.matmul_mx(
                     out=y[h, t][:],
                     lhsT=w_codes[:, P * t : P * (t + 1)].bitcast(FP8X4),
                     lhsT_scale=w_scales[:, P * t : P * (t + 1)],
                     rhs=x_pick[h][:].bitcast(FP8X4),
-                    rhs_scale=s_pick[:, HALF * h : HALF * (h + 1)],
+                    rhs_scale=scale_pick[:, WIDTH * h : WIDTH * (h + 1)],
                     start=True,
                     stop=True,
                 )
 
-        def buf(name, c, width=HALF):
-            return keep.tile([P, width], F32, name="%s%d" % (name, c))
+        out_rows = out.rearrange("(p t) e -> t p e", t=TILES)
+        made = {}
 
-        st = [dict() for c in chunks]
+        def new(name, h, t, width=WIDTH):
+            made[name, h, t] = keep.tile([P, width], F32, name="%s%d%d" % (name, h, t))
+            return made[name, h, t][:]
 
-        def relu(c):
-            h, t = chunks[c]
-            r = buf("r", c)
-            nc.scalar.activation(r[:], y[h, t][:], ACT.Relu, bias=lm_col[:, t : t + 1])
-            st[c].update(r=r)
+        def got(name, h, t):
+            return made[name, h, t][:]
 
-        def square(c):
-            q = buf("q", c)
-            nc.scalar.activation(q[:], st[c]["r"][:], ACT.Square)
-            st[c].update(q=q)
+        def by_run(ap):
+            return ap.rearrange("p (v d) -> p v d", d=D)
 
-        def gain_s(c):
-            h, t = chunks[c]
-            gg = buf("gg", c)
-            nc.scalar.activation(gg[:], st[c]["q"][:], ACT.Copy, scale=sc_col[:, t : t + 1])
-            st[c].update(gg=gg)
+        def store(h, t):
+            nc.sync.dma_start(out_rows[t][:, WIDTH * h : WIDTH * (h + 1)], got("out", h, t))
 
-        def gain_v(c):
-            h, t = chunks[c]
-            gg = buf("gg", c)
-            r = st[c]["r"]
-            nc.vector.scalar_tensor_tensor(gg[:], r[:], sc_col[:, t : t + 1], r[:], ALU.mult, ALU.mult)
-            st[c].update(gg=gg)
+        def relu(h, t):
+            nc.scalar.activation(new("relu", h, t), y[h, t][:], ACT.Relu, bias=lm_col[:, t : t + 1])
 
-        def peak(c):
-            mg = buf("mg", c, HALF // D)
-            nc.vector.tensor_reduce(mg[:], st[c]["gg"][:].rearrange("p (v d) -> p v d", d=D), AX.X, ALU.max)
-            st[c].update(mg=mg)
+        def peak(h, t):
+            nc.vector.tensor_reduce(new("mg", h, t, GROUPS), by_run(got("gg", h, t)), AX.X, ALU.max)
 
-        def sig2(c):
-            s2 = buf("s2", c)
-            nc.scalar.activation(s2[:], st[c]["gg"][:], ACT.Sigmoid, bias=-2.0, scale=4.0)
-            st[c].update(s2=s2)
+        def gap(h, t):
+            pk = got("mg", h, t).unsqueeze(2).to_broadcast([P, GROUPS, D])
+            nc.vector.tensor_tensor(by_run(new("gap", h, t)), by_run(got("gg", h, t)), pk, ALU.subtract)
 
-        def gap(c):
-            gg, mg = st[c]["gg"], st[c]["mg"]
-            d = buf("d", c)
-            nc.vector.tensor_tensor(
-                d[:].rearrange("p (v d) -> p v d", d=D),
-                gg[:].rearrange("p (v d) -> p v d", d=D),
-                mg[:].unsqueeze(2).to_broadcast([P, HALF // D, D]),
-                ALU.subtract,
+        def is_peak(h, t):
+            nc.scalar.activation(new("is_peak", h, t), got("gap", h, t), ACT.Sigmoid, bias=0.8, scale=8.0)
+
+        def is_high(h, t):
+            nc.scalar.activation(new("is_high", h, t), got("gg", h, t), ACT.Sigmoid, bias=-2.0, scale=4.0)
+
+        def gain_on_vector(h, t):
+            nc.vector.scalar_tensor_tensor(
+                new("gg", h, t), got("relu", h, t), sc_col[:, t : t + 1], got("relu", h, t), ALU.mult, ALU.mult
             )
-            st[c].update(d=d)
 
-        def sig1(c):
-            s1 = buf("s1", c)
-            nc.scalar.activation(s1[:], st[c]["d"][:], ACT.Sigmoid, bias=0.8, scale=8.0)
-            st[c].update(s1=s1)
+        def square(h, t):
+            nc.scalar.activation(new("square", h, t), got("relu", h, t), ACT.Square)
 
-        def gate2(c):
-            h, t = chunks[c]
-            u = buf("u", c)
-            nc.vector.scalar_tensor_tensor(u[:], y[h, t][:], lm_col[:, t : t + 1], st[c]["s2"][:], ALU.add, ALU.mult)
-            st[c].update(u=u)
+        def gain_on_scalar(h, t):
+            nc.scalar.activation(new("gg", h, t), got("square", h, t), ACT.Copy, scale=sc_col[:, t : t + 1])
 
-        def gate1(c):
-            h, t = chunks[c]
-            z = buf("z", c)
-            nc.vector.scalar_tensor_tensor(z[:], st[c]["u"][:], sc_col[:, t : t + 1], st[c]["s1"][:], ALU.mult, ALU.mult)
-            st[c].update(z=z)
+        def scaled_on(h, t):
+            nc.vector.scalar_tensor_tensor(
+                new("on_sc", h, t), got("is_peak", h, t), sc_col[:, t : t + 1], got("is_high", h, t), ALU.mult, ALU.mult
+            )
 
-        def gate1g(c):
-            z = buf("z", c)
-            nc.gpsimd.tensor_tensor(z[:], st[c]["u"][:], st[c]["s1"][:], ALU.mult)
-            st[c].update(z=z)
+        def shift(h, t):
+            nc.scalar.activation(new("bl", h, t), y[h, t][:], ACT.Identity, bias=lm_col[:, t : t + 1])
 
-        def rest(c):
-            h, t = chunks[c]
-            o = buf("o", c)
-            nc.vector.tensor_tensor(o[:], y[h, t][:], st[c]["z"][:], ALU.subtract)
-            nc.sync.dma_start(out_rows[t][:, HALF * h : HALF * (h + 1)], o[:])
+        def neg_rest(h, t):
+            nc.vector.scalar_tensor_tensor(
+                new("neg_rest", h, t), got("on_sc", h, t), 1.0, got("bl", h, t), ALU.subtract, ALU.mult
+            )
 
-        def shift(c):
-            h, t = chunks[c]
-            bl = buf("bl", c)
-            nc.scalar.activation(bl[:], y[h, t][:], ACT.Identity, bias=lm_col[:, t : t + 1])
-            st[c].update(bl=bl)
+        def end_on_scalar(h, t):
+            nc.scalar.activation(
+                new("out", h, t), got("neg_rest", h, t), ACT.Identity, bias=neg_lm[:, t : t + 1], scale=-1.0
+            )
+            store(h, t)
 
-        def fire(c):
-            h, t = chunks[c]
-            on = buf("on", c)
-            nc.vector.scalar_tensor_tensor(on[:], st[c]["s1"][:], sc_col[:, t : t + 1], st[c]["s2"][:], ALU.mult, ALU.mult)
-            st[c].update(on=on)
+        def high_bl(h, t):
+            nc.vector.scalar_tensor_tensor(
+                new("high_bl", h, t), y[h, t][:], lm_col[:, t : t + 1], got("is_high", h, t), ALU.add, ALU.mult
+            )
 
-        def keepbl(c):
-            p = buf("p", c)
-            nc.vector.scalar_tensor_tensor(p[:], st[c]["on"][:], 1.0, st[c]["bl"][:], ALU.subtract, ALU.mult)
-            st[c].update(p=p)
+        def spike(h, t):
+            nc.vector.scalar_tensor_tensor(
+                new("spike", h, t), got("high_bl", h, t), sc_col[:, t : t + 1], got("is_peak", h, t), ALU.mult, ALU.mult
+            )
 
-        def unshift(c):
-            h, t = chunks[c]
-            o = buf("o", c)
-            nc.scalar.activation(o[:], st[c]["p"][:], ACT.Identity, bias=neg_lm[:, t : t + 1], scale=-1.0)
-            nc.sync.dma_start(out_rows[t][:, HALF * h : HALF * (h + 1)], o[:])
+        def end_on_vector(h, t):
+            nc.vector.tensor_tensor(new("out", h, t), y[h, t][:], got("spike", h, t), ALU.subtract)
+            store(h, t)
 
-        A, B = (0, 1), (2, 3)
-        for stage, group in [(relu, A), (gain_v, A), (relu, B), (peak, A), (square, B), (gap, A), (gain_s, B), (peak, B), (sig2, A), (gap, B), (sig1, A), (fire, A), (shift, A), (keepbl, A), (sig2, B), (gate2, B), (sig1, B), (gate1, B), (unshift, A), (rest, B)]:
-            for c in group:
-                stage(c)
+        def both_tiles(step, h):
+            for t in range(TILES):
+                step(h, t)
+
+        first, second = range(HALVES)
+        both_tiles(relu, first)
+        both_tiles(gain_on_vector, first)
+        both_tiles(relu, second)
+        both_tiles(peak, first)
+        both_tiles(square, second)
+        both_tiles(gap, first)
+        both_tiles(gain_on_scalar, second)
+        both_tiles(peak, second)
+        both_tiles(is_high, first)
+        both_tiles(gap, second)
+        both_tiles(is_peak, first)
+        both_tiles(scaled_on, first)
+        both_tiles(shift, first)
+        both_tiles(neg_rest, first)
+        both_tiles(is_high, second)
+        both_tiles(high_bl, second)
+        both_tiles(is_peak, second)
+        both_tiles(spike, second)
+        both_tiles(end_on_scalar, first)
+        both_tiles(end_on_vector, second)

from contextlib import ExitStack

import concourse.mybir as mybir

K, T, S, D, N = 512, 2048, 512, 4, 256
FLOPS = 2 * K * N * S

F32 = mybir.dt.float32
BF16 = mybir.dt.bfloat16
I32 = mybir.dt.int32
U32 = mybir.dt.uint32
U16 = mybir.dt.uint16
U8 = mybir.dt.uint8
FP8X4 = mybir.dt.float8_e4m3fn_x4
ALU = mybir.AluOpType
ACT = mybir.ActivationFunctionType
AX = mybir.AxisListType

P = 128
PACK = 4
QUADRANT = 32
SCALE_ROWS = 4
TILES = N // P
HALVES = 2
WIDTH = S // HALVES
GROUPS = WIDTH // D
LIST_ROWS = 16
LIST_COLUMNS = WIDTH // LIST_ROWS
NEIGHBOURS = 2
MX_ALIGN = 64


def tile_picked_yspike_rest_p_kernel(tc, x_words, x_scales, w1, lm, sc, offs, out):
    nc = tc.nc
    with ExitStack() as ctx:
        keep = ctx.enter_context(tc.tile_pool(name="keep", bufs=1))
        psum = ctx.enter_context(tc.psum_pool(name="psum", bufs=1))

        offsets = keep.tile([P, S // LIST_ROWS], U16, name="offsets")
        w_raw = keep.tile([P, PACK, N], F32, name="w_raw")
        x_table = keep.tile([P, T], I32, name="x_table", align_bytes=MX_ALIGN)
        scale_table = keep.tile([P, T], U8, name="scale_table", tag="scale_slot", align_bytes=MX_ALIGN)
        lm_col = keep.tile([P, TILES], F32, name="lm_col")
        sc_col = keep.tile([P, TILES], F32, name="sc_col")
        warm_in = keep.tile([P, 1], F32, name="warm_in")
        warm_out = keep.tile([P, 1], F32, name="warm_out")

        nc.vector.memset(scale_table[:].bitcast(I32), 0)

        nc.vector.memset(warm_in[:], 0.0)
        nc.scalar.activation(warm_out[:], warm_in[:], ACT.Sigmoid)

        nc.sync.dma_start(w_raw[:], w1.rearrange("(p j) m -> p j m", j=PACK))
        nc.sync.dma_start(offsets[:], offs)
        scale_rows = x_scales[0].rearrange("(q r) c -> r q c", r=SCALE_ROWS)
        for r in range(SCALE_ROWS):
            nc.sync.dma_start(scale_table[r:P:QUADRANT, :].bitcast(I32), scale_rows[r].bitcast(I32))
        nc.sync.dma_start(x_table[:], x_words[0].rearrange("p c j -> p (c j)").bitcast(I32))
        nc.sync.dma_start(lm_col[:], lm.rearrange("(p t) o -> p (t o)", t=TILES))
        nc.sync.dma_start(sc_col[:], sc.rearrange("(p t) o -> p (t o)", t=TILES))

        w_bf = keep.tile([P, N, PACK], BF16, name="w_bf", align_bytes=MX_ALIGN)
        w_codes = keep.tile([P, N], U32, name="w_codes", align_bytes=MX_ALIGN)
        nc.scalar.copy(
            w_bf[:].rearrange("p (t g i) j -> p g j i t", t=TILES, i=NEIGHBOURS),
            w_raw[:].rearrange("p j (g i t) -> p g j i t", t=TILES, i=NEIGHBOURS),
        )
        scale_pick = keep.tile([P, S], U8, name="scale_pick", align_bytes=MX_ALIGN)
        nc.vector.tensor_copy(scale_pick[:], scale_table[:].indirect(offsets[:]))

        w_scales = keep.tile([P, N], U8, name="w_scales", tag="scale_slot", align_bytes=MX_ALIGN)
        nc.vector.quantize_mx(
            out=w_codes[:].bitcast(FP8X4), scales=w_scales[:], in_=w_bf[:].rearrange("p m j -> p (m j)")
        )

        neg_lm = keep.tile([P, TILES], F32, name="neg_lm")
        nc.scalar.activation(neg_lm[:], lm_col[:], ACT.Copy, scale=-1.0)

        x_pick = [keep.tile([P, WIDTH], U32, name="x_pick%d" % h, align_bytes=MX_ALIGN) for h in range(HALVES)]
        y = {}
        for h in range(HALVES):
            half_list = offsets[:, LIST_COLUMNS * h : LIST_COLUMNS * (h + 1)]
            nc.vector.tensor_copy(x_pick[h][:], x_table[:].bitcast(U32).indirect(half_list))
            for t in range(TILES):
                y[h, t] = psum.tile([P, WIDTH], F32, name="y%d%d" % (h, t))
                nc.tensor.matmul_mx(
                    out=y[h, t][:],
                    lhsT=w_codes[:, P * t : P * (t + 1)].bitcast(FP8X4),
                    lhsT_scale=w_scales[:, P * t : P * (t + 1)],
                    rhs=x_pick[h][:].bitcast(FP8X4),
                    rhs_scale=scale_pick[:, WIDTH * h : WIDTH * (h + 1)],
                    start=True,
                    stop=True,
                )

        out_rows = out.rearrange("(p t) e -> t p e", t=TILES)
        made = {}

        def new(name, h, t, width=WIDTH):
            made[name, h, t] = keep.tile([P, width], F32, name="%s%d%d" % (name, h, t))
            return made[name, h, t][:]

        def got(name, h, t):
            return made[name, h, t][:]

        def by_run(ap):
            return ap.rearrange("p (v d) -> p v d", d=D)

        def store(h, t):
            nc.sync.dma_start(out_rows[t][:, WIDTH * h : WIDTH * (h + 1)], got("out", h, t))

        def relu(h, t):
            nc.scalar.activation(new("relu", h, t), y[h, t][:], ACT.Relu, bias=lm_col[:, t : t + 1])

        def peak(h, t):
            nc.vector.tensor_reduce(new("mg", h, t, GROUPS), by_run(got("gg", h, t)), AX.X, ALU.max)

        def gap(h, t):
            pk = got("mg", h, t).unsqueeze(2).to_broadcast([P, GROUPS, D])
            nc.vector.tensor_tensor(by_run(new("gap", h, t)), by_run(got("gg", h, t)), pk, ALU.subtract)

        def is_peak(h, t):
            nc.scalar.activation(new("is_peak", h, t), got("gap", h, t), ACT.Sigmoid, bias=0.8, scale=8.0)

        def is_high(h, t):
            nc.scalar.activation(new("is_high", h, t), got("gg", h, t), ACT.Sigmoid, bias=-2.0, scale=4.0)

        def gain_on_vector(h, t):
            nc.vector.scalar_tensor_tensor(
                new("gg", h, t), got("relu", h, t), sc_col[:, t : t + 1], got("relu", h, t), ALU.mult, ALU.mult
            )

        def square(h, t):
            nc.scalar.activation(new("square", h, t), got("relu", h, t), ACT.Square)

        def gain_on_scalar(h, t):
            nc.scalar.activation(new("gg", h, t), got("square", h, t), ACT.Copy, scale=sc_col[:, t : t + 1])

        def scaled_on(h, t):
            nc.vector.scalar_tensor_tensor(
                new("on_sc", h, t), got("is_peak", h, t), sc_col[:, t : t + 1], got("is_high", h, t), ALU.mult, ALU.mult
            )

        def shift(h, t):
            nc.scalar.activation(new("bl", h, t), y[h, t][:], ACT.Identity, bias=lm_col[:, t : t + 1])

        def neg_rest(h, t):
            nc.vector.scalar_tensor_tensor(
                new("neg_rest", h, t), got("on_sc", h, t), 1.0, got("bl", h, t), ALU.subtract, ALU.mult
            )

        def end_on_scalar(h, t):
            nc.scalar.activation(
                new("out", h, t), got("neg_rest", h, t), ACT.Identity, bias=neg_lm[:, t : t + 1], scale=-1.0
            )
            store(h, t)

        def high_bl(h, t):
            nc.vector.scalar_tensor_tensor(
                new("high_bl", h, t), y[h, t][:], lm_col[:, t : t + 1], got("is_high", h, t), ALU.add, ALU.mult
            )

        def spike(h, t):
            nc.vector.scalar_tensor_tensor(
                new("spike", h, t), got("high_bl", h, t), sc_col[:, t : t + 1], got("is_peak", h, t), ALU.mult, ALU.mult
            )

        def end_on_vector(h, t):
            nc.vector.tensor_tensor(new("out", h, t), y[h, t][:], got("spike", h, t), ALU.subtract)
            store(h, t)

        def both_tiles(step, h):
            for t in range(TILES):
                step(h, t)

        first, second = range(HALVES)
        both_tiles(relu, first)
        both_tiles(gain_on_vector, first)
        both_tiles(relu, second)
        both_tiles(peak, first)
        both_tiles(square, second)
        both_tiles(gap, first)
        both_tiles(gain_on_scalar, second)
        both_tiles(peak, second)
        both_tiles(is_high, first)
        both_tiles(gap, second)
        both_tiles(is_peak, first)
        both_tiles(scaled_on, first)
        both_tiles(shift, first)
        both_tiles(neg_rest, first)
        both_tiles(is_high, second)
        both_tiles(high_bl, second)
        both_tiles(is_peak, second)
        both_tiles(spike, second)
        both_tiles(end_on_scalar, first)
        both_tiles(end_on_vector, second)
